import numpy as np
import ml_dtypes


def mxq(x, axis, fmt="e4m3"):
    dtype, down = {"e4m3": (ml_dtypes.float8_e4m3fn, 7), "e5m2": (ml_dtypes.float8_e5m2, 14)}[fmt]
    v = np.moveaxis(np.asarray(x, np.float32).astype(ml_dtypes.bfloat16).astype(np.float64), axis, -1)
    blocks = v.reshape(v.shape[:-1] + (-1, 32))
    amax = np.abs(blocks).max(-1, keepdims=True)
    byte = np.maximum(np.where(amax > 0, np.frexp(amax)[1] - 1 + 127, 0) - down, 1)
    scale = np.exp2(byte - 127.0)
    codes = (blocks / scale).astype(np.float32).astype(dtype).astype(np.float64)
    return np.moveaxis((codes * scale).reshape(v.shape), -1, axis)


WIDE = False


def mx_kscale(k, group=512):
    if not WIDE:
        return np.ones(k)
    levels = np.array([18, -18])
    if group != 512:
        return np.exp2(np.random.permutation(np.resize(levels, k // group))).repeat(group)
    if k % 512:
        return np.exp2(np.random.permutation(np.resize(levels, k // 32))).repeat(32)
    a = np.empty((k // 512, 16))
    for p in range(k // 512):
        a[p, :8] = np.random.permutation(np.resize(levels, 8))
        for g in range(8):
            far = levels[np.abs(levels - a[p, g]) >= 10]
            a[p, g + 8] = far[np.random.randint(len(far))]
    return np.exp2(a.ravel()).repeat(32)


def f64(x):
    return np.asarray(x).astype(np.float64)


def sigmoid(v):
    return 1.0 / (1.0 + np.exp(-v))


G, D, M, N = 4, 128, 128, 512


def setup_inputs():
    n = np.random.standard_normal
    s_d = mx_kscale(D, 0)
    return {
        "h": (n((G, D, N)) * s_d[:, None]).astype(np.float32),
        "wt": (n((G, D, M)) / np.sqrt(D) / s_d[:, None]).astype(np.float32),
        "wc": (n((G, D, M)) / np.sqrt(D) / s_d[:, None]).astype(np.float32),
        "xr": (n((G, M, N))).astype(np.float32),
        "bt": (0.5 * n((G, M, 1))).astype(np.float32),
        "bc": (0.5 * n((G, M, 1))).astype(np.float32),
    }


def reference(h, wt, wc, xr, bt, bc):
    wtq = mxq(f64(wt), 1, "e4m3")
    hq = mxq(f64(h), 1, "e4m3")
    zt = wtq.transpose(0, 2, 1) @ hq
    wcq = mxq(f64(wc), 1, "e4m3")
    zc = wcq.transpose(0, 2, 1) @ hq
    t = sigmoid(zt + f64(bt))
    y = t * np.maximum(zc + f64(bc), 0.0) + (1.0 - t) * f64(xr)
    return y

@@ -1,0 +1,166 @@
+from contextlib import ExitStack
+
+import concourse.mybir as mybir
+
+G, D, M, N = 4, 128, 128, 512
+FLOPS = 2 * 2 * G * D * M * N
+
+F32 = mybir.dt.float32
+BF16 = mybir.dt.bfloat16
+U32 = mybir.dt.uint32
+U8 = mybir.dt.uint8
+FP8X4 = mybir.dt.float8_e4m3fn_x4
+ALU = mybir.AluOpType
+ACT = mybir.ActivationFunctionType
+
+P = 128
+PACK = 4
+ROWS = D // PACK
+HALF = N // 2
+N_MM = 128
+RUN = 4
+SQ = 32
+
+
+def tile_rows_cell_hwy_kernel(tc, h, wt, wc, xr, bt, bc, out):
+    nc = tc.nc
+    with ExitStack() as ctx:
+        sb = ctx.enter_context(tc.tile_pool(name="sb", bufs=1))
+        ps = ctx.enter_context(tc.psum_pool(name="ps", bufs=1))
+        ctx.enter_context(tc.manual_schedule())
+
+        def operand(name, width):
+            raw = sb.tile([P, PACK, width], F32, name=name + "_raw", align_bytes=64)
+            packed = sb.tile([P, width, PACK], BF16, name=name + "_bf16", align_bytes=64)
+            codes = sb.tile([P, width], U32, name=name + "_codes", align_bytes=64)
+            scales = sb.tile([P, width], U8, name=name + "_scales", align_bytes=64)
+            return raw, packed, codes, scales
+
+        h_ops = [operand("h%d" % c, HALF) for c in range(2)]
+        wt_op = operand("wt", M)
+        wc_op = operand("wc", M)
+        x_sb = [sb.tile([P, N], F32, name="x%d" % g) for g in range(G)]
+        t_sb = [sb.tile([P, N], F32, name="t%d" % g) for g in range(G)]
+        u_sb = [sb.tile([P, N], F32, name="u%d" % g) for g in range(G)]
+        v_sb = [sb.tile([P, N], F32, name="v%d" % g) for g in range(G)]
+        y_sb = [sb.tile([P, N], F32, name="y%d" % g) for g in range(G)]
+        zt = [ps.tile([P, N], F32, name="zt%d" % g) for g in range(G)]
+        zc = [ps.tile([P, N], F32, name="zc%d" % g) for g in range(G)]
+        bias_rows = sb.tile([P, G * SQ], F32, align_bytes=64)
+        bias = sb.tile([P, G * SQ], F32, align_bytes=64)
+
+        def cols(c):
+            return slice(c * HALF, (c + 1) * HALF)
+
+        def load_operand(op, src):
+            nc.sync.dma_start(out=op[0][:], in_=src)
+
+        def by_rows(a):
+            return a.rearrange("g (p j) w -> (g p) j w", j=PACK)
+
+        def interleave(copy, op):
+            copy(
+                out=op[1][:].rearrange("p (c i) j -> p c j i", i=RUN),
+                in_=op[0][:].rearrange("p j (c i) -> p c j i", i=RUN),
+            )
+
+        def quantise(op):
+            nc.vector.quantize_mx(
+                out=op[2][:].bitcast(FP8X4),
+                scales=op[3][:],
+                in_=op[1][:].rearrange("p w j -> p (w j)"),
+            )
+
+        def product(acc, w_op, c, g):
+            rows = slice(g * ROWS, (g + 1) * ROWS)
+            for n0 in range(0, HALF, N_MM):
+                nc.tensor.matmul_mx(
+                    out=acc[g][:, c * HALF + n0 : c * HALF + n0 + N_MM],
+                    lhsT=w_op[2][rows, :].bitcast(FP8X4),
+                    lhsT_scale=w_op[3][rows, :],
+                    rhs=h_ops[c][2][rows, n0 : n0 + N_MM].bitcast(FP8X4),
+                    rhs_scale=h_ops[c][3][rows, n0 : n0 + N_MM],
+                    start=True,
+                    stop=True,
+                )
+
+        def gate(c, g):
+            nc.scalar.activation(
+                out=t_sb[g][:, cols(c)], in_=zt[g][:, cols(c)], func=ACT.Sigmoid,
+                bias=bias[:, g * SQ : g * SQ + 1],
+            )
+
+        def transform(c, g):
+            nc.vector.scalar_tensor_tensor(
+                out=u_sb[g][:, cols(c)], in0=zc[g][:, cols(c)],
+                scalar=bias[:, g * SQ + 1 : g * SQ + 2], in1=t_sb[g][:, cols(c)],
+                op0=ALU.add, op1=ALU.mult,
+            )
+
+        def carry(c, g):
+            nc.vector.scalar_tensor_tensor(
+                out=v_sb[g][:, cols(c)], in0=t_sb[g][:, cols(c)], scalar=1.0,
+                in1=x_sb[g][:, cols(c)], op0=ALU.subtract, op1=ALU.mult,
+            )
+
+        def combine(c, g):
+            nc.vector.scalar_tensor_tensor(
+                out=y_sb[g][:, cols(c)], in0=u_sb[g][:, cols(c)], scalar=0.0,
+                in1=v_sb[g][:, cols(c)], op0=ALU.max, op1=ALU.subtract,
+            )
+            nc.sync.dma_start(out=out[g, :, cols(c)], in_=y_sb[g][:, cols(c)])
+
+        nc.vector.memset(bias_rows[:], 0.0)
+        for r, b in enumerate((bt, bc)):
+            nc.scalar.dma_start(
+                out=bias_rows[r:P:SQ, :].rearrange("q (g i) -> q g i", i=SQ),
+                in_=b.rearrange("g (q i) o -> q g (i o)", i=SQ),
+            )
+        load_operand(h_ops[0], by_rows(h)[:, :, cols(0)])
+        load_operand(wt_op, by_rows(wt))
+        load_operand(wc_op, by_rows(wc))
+        nc.sync.dma_start(out=x_sb[0][:], in_=xr[0])
+        load_operand(h_ops[1], by_rows(h)[:, :, cols(1)])
+        for g in range(1, G):
+            nc.sync.dma_start(out=x_sb[g][:], in_=xr[g])
+
+        nc.vector.transpose(out=bias[:], in_=bias_rows[:])
+        interleave(nc.vector.tensor_copy, h_ops[0])
+        interleave(nc.vector.tensor_copy, wt_op)
+        quantise(h_ops[0])
+        quantise(wt_op)
+        interleave(nc.vector.tensor_copy, wc_op)
+        for g in range(G):
+            product(zt, wt_op, 0, g)
+            gate(0, g)
+        quantise(wc_op)
+        for g in range(G):
+            product(zc, wc_op, 0, g)
+        interleave(nc.scalar.copy, h_ops[1])
+
+        carry(0, 0)
+        transform(0, 0)
+        transform(0, 1)
+        combine(0, 0)
+        transform(0, 2)
+        carry(0, 1)
+        transform(0, 3)
+        quantise(h_ops[1])
+        for g in range(G):
+            product(zt, wt_op, 1, g)
+            gate(1, g)
+        for g in range(G):
+            product(zc, wc_op, 1, g)
+        combine(0, 1)
+        carry(0, 2)
+        carry(0, 3)
+        combine(0, 2)
+        combine(0, 3)
+
+        carry(1, 0)
+        transform(1, 0)
+        for g in range(1, G):
+            carry(1, g)
+            transform(1, g)
+            combine(1, g - 1)
+        combine(1, G - 1)

@@ -111,12 +111,12 @@ def tile_rows_cell_hwy_kernel(tc, h, wt, wc, xr, bt, bc, out):
             nc.sync.dma_start(out=out[g, :, cols(c)], in_=y_sb[g][:, cols(c)])
 
         nc.vector.memset(bias_rows[:], 0.0)
+        load_operand(h_ops[0], by_rows(h)[:, :, cols(0)])
         for r, b in enumerate((bt, bc)):
-            nc.scalar.dma_start(
+            nc.sync.dma_start(
                 out=bias_rows[r:P:SQ, :].rearrange("q (g i) -> q g i", i=SQ),
                 in_=b.rearrange("g (q i) o -> q g (i o)", i=SQ),
             )
-        load_operand(h_ops[0], by_rows(h)[:, :, cols(0)])
         load_operand(wt_op, by_rows(wt))
         load_operand(wc_op, by_rows(wc))
         nc.sync.dma_start(out=x_sb[0][:], in_=xr[0])
@@ -124,8 +124,8 @@ def tile_rows_cell_hwy_kernel(tc, h, wt, wc, xr, bt, bc, out):
         for g in range(1, G):
             nc.sync.dma_start(out=x_sb[g][:], in_=xr[g])
 
-        nc.vector.transpose(out=bias[:], in_=bias_rows[:])
         interleave(nc.vector.tensor_copy, h_ops[0])
+        nc.vector.transpose(out=bias[:], in_=bias_rows[:])
         interleave(nc.vector.tensor_copy, wt_op)
         quantise(h_ops[0])
         quantise(wt_op)

@@ -20,6 +20,8 @@ HALF = N // 2
 N_MM = 128
 RUN = 4
 SQ = 32
+H_SPLIT = 192
+W_SPLIT = 80
 
 
 def tile_rows_cell_hwy_kernel(tc, h, wt, wc, xr, bt, bc, out):
@@ -58,10 +60,10 @@ def tile_rows_cell_hwy_kernel(tc, h, wt, wc, xr, bt, bc, out):
         def by_rows(a):
             return a.rearrange("g (p j) w -> (g p) j w", j=PACK)
 
-        def interleave(copy, op):
+        def interleave(copy, op, w0, w1):
             copy(
-                out=op[1][:].rearrange("p (c i) j -> p c j i", i=RUN),
-                in_=op[0][:].rearrange("p j (c i) -> p c j i", i=RUN),
+                out=op[1][:, w0:w1, :].rearrange("p (c i) j -> p c j i", i=RUN),
+                in_=op[0][:, :, w0:w1].rearrange("p j (c i) -> p c j i", i=RUN),
             )
 
         def quantise(op):
@@ -110,33 +112,44 @@ def tile_rows_cell_hwy_kernel(tc, h, wt, wc, xr, bt, bc, out):
             )
             nc.sync.dma_start(out=out[g, :, cols(c)], in_=y_sb[g][:, cols(c)])
 
+        warm = sb.tile([P, 1], F32)
+        nc.gpsimd.memset(warm[:], 0.0)
+        nc.scalar.activation(out=warm[:], in_=warm[:], func=ACT.Sigmoid)
         nc.vector.memset(bias_rows[:], 0.0)
         load_operand(h_ops[0], by_rows(h)[:, :, cols(0)])
+        load_operand(wt_op, by_rows(wt))
+        load_operand(wc_op, by_rows(wc))
         for r, b in enumerate((bt, bc)):
             nc.sync.dma_start(
                 out=bias_rows[r:P:SQ, :].rearrange("q (g i) -> q g i", i=SQ),
                 in_=b.rearrange("g (q i) o -> q g (i o)", i=SQ),
             )
-        load_operand(wt_op, by_rows(wt))
-        load_operand(wc_op, by_rows(wc))
         nc.sync.dma_start(out=x_sb[0][:], in_=xr[0])
         load_operand(h_ops[1], by_rows(h)[:, :, cols(1)])
         for g in range(1, G):
             nc.sync.dma_start(out=x_sb[g][:], in_=xr[g])
 
-        interleave(nc.vector.tensor_copy, h_ops[0])
-        nc.vector.transpose(out=bias[:], in_=bias_rows[:])
-        interleave(nc.vector.tensor_copy, wt_op)
+        def interleave_shared(op, split, width):
+            interleave(nc.vector.tensor_copy, op, 0, split)
+            interleave(nc.scalar.copy, op, split, width)
+
+        interleave_shared(h_ops[0], H_SPLIT, HALF)
+        interleave_shared(wt_op, W_SPLIT, M)
         quantise(h_ops[0])
         quantise(wt_op)
-        interleave(nc.vector.tensor_copy, wc_op)
-        for g in range(G):
+        interleave_shared(wc_op, W_SPLIT, M)
+        nc.vector.transpose(out=bias[:], in_=bias_rows[:])
+        quantise(wc_op)
+        for g in range(G - 1):
             product(zt, wt_op, 0, g)
             gate(0, g)
-        quantise(wc_op)
-        for g in range(G):
-            product(zc, wc_op, 0, g)
-        interleave(nc.scalar.copy, h_ops[1])
+        interleave(nc.scalar.copy, h_ops[1], 0, HALF)
+        product(zc, wc_op, 0, 0)
+        product(zc, wc_op, 0, 1)
+        product(zt, wt_op, 0, 3)
+        gate(0, 3)
+        product(zc, wc_op, 0, 2)
+        product(zc, wc_op, 0, 3)
 
         carry(0, 0)
         transform(0, 0)
@@ -144,15 +157,14 @@ def tile_rows_cell_hwy_kernel(tc, h, wt, wc, xr, bt, bc, out):
         combine(0, 0)
         transform(0, 2)
         carry(0, 1)
-        transform(0, 3)
         quantise(h_ops[1])
+        combine(0, 1)
+        carry(0, 2)
+        transform(0, 3)
         for g in range(G):
             product(zt, wt_op, 1, g)
             gate(1, g)
-        for g in range(G):
             product(zc, wc_op, 1, g)
-        combine(0, 1)
-        carry(0, 2)
         carry(0, 3)
         combine(0, 2)
         combine(0, 3)

from contextlib import ExitStack

import concourse.mybir as mybir

G, D, M, N = 4, 128, 128, 512
FLOPS = 2 * 2 * G * D * M * N

F32 = mybir.dt.float32
BF16 = mybir.dt.bfloat16
U32 = mybir.dt.uint32
U8 = mybir.dt.uint8
FP8X4 = mybir.dt.float8_e4m3fn_x4
ALU = mybir.AluOpType
ACT = mybir.ActivationFunctionType

P = 128
PACK = 4
ROWS = D // PACK
HALF = N // 2
N_MM = 128
RUN = 4
SQ = 32
H_SPLIT = 192
W_SPLIT = 80


def tile_rows_cell_hwy_kernel(tc, h, wt, wc, xr, bt, bc, out):
    nc = tc.nc
    with ExitStack() as ctx:
        sb = ctx.enter_context(tc.tile_pool(name="sb", bufs=1))
        ps = ctx.enter_context(tc.psum_pool(name="ps", bufs=1))
        ctx.enter_context(tc.manual_schedule())

        def operand(name, width):
            raw = sb.tile([P, PACK, width], F32, name=name + "_raw", align_bytes=64)
            packed = sb.tile([P, width, PACK], BF16, name=name + "_bf16", align_bytes=64)
            codes = sb.tile([P, width], U32, name=name + "_codes", align_bytes=64)
            scales = sb.tile([P, width], U8, name=name + "_scales", align_bytes=64)
            return raw, packed, codes, scales

        h_ops = [operand("h%d" % c, HALF) for c in range(2)]
        wt_op = operand("wt", M)
        wc_op = operand("wc", M)
        x_sb = [sb.tile([P, N], F32, name="x%d" % g) for g in range(G)]
        t_sb = [sb.tile([P, N], F32, name="t%d" % g) for g in range(G)]
        u_sb = [sb.tile([P, N], F32, name="u%d" % g) for g in range(G)]
        v_sb = [sb.tile([P, N], F32, name="v%d" % g) for g in range(G)]
        y_sb = [sb.tile([P, N], F32, name="y%d" % g) for g in range(G)]
        zt = [ps.tile([P, N], F32, name="zt%d" % g) for g in range(G)]
        zc = [ps.tile([P, N], F32, name="zc%d" % g) for g in range(G)]
        bias_rows = sb.tile([P, G * SQ], F32, align_bytes=64)
        bias = sb.tile([P, G * SQ], F32, align_bytes=64)

        def cols(c):
            return slice(c * HALF, (c + 1) * HALF)

        def load_operand(op, src):
            nc.sync.dma_start(out=op[0][:], in_=src)

        def by_rows(a):
            return a.rearrange("g (p j) w -> (g p) j w", j=PACK)

        def interleave(copy, op, w0, w1):
            copy(
                out=op[1][:, w0:w1, :].rearrange("p (c i) j -> p c j i", i=RUN),
                in_=op[0][:, :, w0:w1].rearrange("p j (c i) -> p c j i", i=RUN),
            )

        def quantise(op):
            nc.vector.quantize_mx(
                out=op[2][:].bitcast(FP8X4),
                scales=op[3][:],
                in_=op[1][:].rearrange("p w j -> p (w j)"),
            )

        def product(acc, w_op, c, g):
            rows = slice(g * ROWS, (g + 1) * ROWS)
            for n0 in range(0, HALF, N_MM):
                nc.tensor.matmul_mx(
                    out=acc[g][:, c * HALF + n0 : c * HALF + n0 + N_MM],
                    lhsT=w_op[2][rows, :].bitcast(FP8X4),
                    lhsT_scale=w_op[3][rows, :],
                    rhs=h_ops[c][2][rows, n0 : n0 + N_MM].bitcast(FP8X4),
                    rhs_scale=h_ops[c][3][rows, n0 : n0 + N_MM],
                    start=True,
                    stop=True,
                )

        def gate(c, g):
            nc.scalar.activation(
                out=t_sb[g][:, cols(c)], in_=zt[g][:, cols(c)], func=ACT.Sigmoid,
                bias=bias[:, g * SQ : g * SQ + 1],
            )

        def transform(c, g):
            nc.vector.scalar_tensor_tensor(
                out=u_sb[g][:, cols(c)], in0=zc[g][:, cols(c)],
                scalar=bias[:, g * SQ + 1 : g * SQ + 2], in1=t_sb[g][:, cols(c)],
                op0=ALU.add, op1=ALU.mult,
            )

        def carry(c, g):
            nc.vector.scalar_tensor_tensor(
                out=v_sb[g][:, cols(c)], in0=t_sb[g][:, cols(c)], scalar=1.0,
                in1=x_sb[g][:, cols(c)], op0=ALU.subtract, op1=ALU.mult,
            )

        def combine(c, g):
            nc.vector.scalar_tensor_tensor(
                out=y_sb[g][:, cols(c)], in0=u_sb[g][:, cols(c)], scalar=0.0,
                in1=v_sb[g][:, cols(c)], op0=ALU.max, op1=ALU.subtract,
            )
            nc.sync.dma_start(out=out[g, :, cols(c)], in_=y_sb[g][:, cols(c)])

        warm = sb.tile([P, 1], F32)
        nc.gpsimd.memset(warm[:], 0.0)
        nc.scalar.activation(out=warm[:], in_=warm[:], func=ACT.Sigmoid)
        nc.vector.memset(bias_rows[:], 0.0)
        load_operand(h_ops[0], by_rows(h)[:, :, cols(0)])
        load_operand(wt_op, by_rows(wt))
        load_operand(wc_op, by_rows(wc))
        for r, b in enumerate((bt, bc)):
            nc.sync.dma_start(
                out=bias_rows[r:P:SQ, :].rearrange("q (g i) -> q g i", i=SQ),
                in_=b.rearrange("g (q i) o -> q g (i o)", i=SQ),
            )
        nc.sync.dma_start(out=x_sb[0][:], in_=xr[0])
        load_operand(h_ops[1], by_rows(h)[:, :, cols(1)])
        for g in range(1, G):
            nc.sync.dma_start(out=x_sb[g][:], in_=xr[g])

        def interleave_shared(op, split, width):
            interleave(nc.vector.tensor_copy, op, 0, split)
            interleave(nc.scalar.copy, op, split, width)

        interleave_shared(h_ops[0], H_SPLIT, HALF)
        interleave_shared(wt_op, W_SPLIT, M)
        quantise(h_ops[0])
        quantise(wt_op)
        interleave_shared(wc_op, W_SPLIT, M)
        nc.vector.transpose(out=bias[:], in_=bias_rows[:])
        quantise(wc_op)
        for g in range(G - 1):
            product(zt, wt_op, 0, g)
            gate(0, g)
        interleave(nc.scalar.copy, h_ops[1], 0, HALF)
        product(zc, wc_op, 0, 0)
        product(zc, wc_op, 0, 1)
        product(zt, wt_op, 0, 3)
        gate(0, 3)
        product(zc, wc_op, 0, 2)
        product(zc, wc_op, 0, 3)

        carry(0, 0)
        transform(0, 0)
        transform(0, 1)
        combine(0, 0)
        transform(0, 2)
        carry(0, 1)
        quantise(h_ops[1])
        combine(0, 1)
        carry(0, 2)
        transform(0, 3)
        for g in range(G):
            product(zt, wt_op, 1, g)
            gate(1, g)
            product(zc, wc_op, 1, g)
        carry(0, 3)
        combine(0, 2)
        combine(0, 3)

        carry(1, 0)
        transform(1, 0)
        for g in range(1, G):
            carry(1, g)
            transform(1, g)
            combine(1, g - 1)
        combine(1, G - 1)
